import numpy as np
import ml_dtypes


def mxq(x, axis, fmt="e4m3"):
    dtype, down = {"e4m3": (ml_dtypes.float8_e4m3fn, 7), "e5m2": (ml_dtypes.float8_e5m2, 14)}[fmt]
    v = np.moveaxis(np.asarray(x, np.float32).astype(ml_dtypes.bfloat16).astype(np.float64), axis, -1)
    blocks = v.reshape(v.shape[:-1] + (-1, 32))
    amax = np.abs(blocks).max(-1, keepdims=True)
    byte = np.maximum(np.where(amax > 0, np.frexp(amax)[1] - 1 + 127, 0) - down, 1)
    scale = np.exp2(byte - 127.0)
    codes = (blocks / scale).astype(np.float32).astype(dtype).astype(np.float64)
    return np.moveaxis((codes * scale).reshape(v.shape), -1, axis)


WIDE = False


def mx_kscale(k):
    if not WIDE:
        return np.ones(k)
    levels = np.array([30, -30])
    if k % 512:
        return np.exp2(np.random.permutation(np.resize(levels, k // 32))).repeat(32)
    a = np.empty((k // 512, 16))
    for p in range(k // 512):
        a[p, :8] = np.random.permutation(np.resize(levels, 8))
        for g in range(8):
            far = levels[np.abs(levels - a[p, g]) >= 10]
            a[p, g + 8] = far[np.random.randint(len(far))]
    return np.exp2(a.ravel()).repeat(32)


def f64(x):
    return np.asarray(x).astype(np.float64)


def striped(idx):
    return np.tile(np.asarray(idx).reshape(-1, 16).T, (8, 1)).astype(np.uint16)


def unstriped(offs):
    return offs[:16].T.reshape(-1).astype(np.int64)


E2M1 = np.array([0.0, 0.5, 1.0, 1.5, 2.0, 3.0, 4.0, 6.0, -0.0, -0.5, -1.0, -1.5, -2.0, -3.0, -4.0, -6.0])


def pack_weight(w, fmt):
    k, n = w.shape
    w = f64(np.asarray(w, np.float32).astype(ml_dtypes.bfloat16)).reshape(k // 32, 32, n)
    amax = np.abs(w).max(1)
    if fmt in ("e4m3", "e5m2"):
        byte = np.frexp(amax)[1] - 1 + 127 - (7 if fmt == "e4m3" else 14)
    else:
        mant, ex = np.frexp(amax / 6.0)
        byte = np.where(mant > 0.5, ex, ex - 1) + 127
    byte = np.clip(np.where(amax > 0, byte, 1), 1, 254)
    scaled = (w * np.exp2(127.0 - byte)[:, None, :]).reshape(k, n).astype(np.float32)
    by_word = np.ascontiguousarray(scaled.reshape(k // 512, 128, 4, n).transpose(0, 1, 3, 2))
    if fmt in ("e4m3", "e5m2"):
        words = by_word.astype(ml_dtypes.float8_e4m3fn if fmt == "e4m3" else ml_dtypes.float8_e5m2).view(np.uint8)
    else:
        c = by_word.astype(ml_dtypes.float4_e2m1fn).view(np.uint8) & 0xF
        words = (c[..., 0::2] | (c[..., 1::2] << 4)).reshape(k // 512, 128, 2 * n)
    return np.ascontiguousarray(words), np.ascontiguousarray(byte.astype(np.uint8).reshape(k // 512, 16, n))


def unpack_weight(words, scales, fmt):
    g, _, n = scales.shape
    words = np.ascontiguousarray(words).reshape(g, 128, n, -1)
    if fmt in ("e4m3", "e5m2"):
        vals = words.view(ml_dtypes.float8_e4m3fn if fmt == "e4m3" else ml_dtypes.float8_e5m2).astype(np.float64)
    else:
        nib = np.empty((g, 128, n, 4), np.uint8)
        nib[..., 0::2] = words & 0xF
        nib[..., 1::2] = words >> 4
        vals = E2M1[nib]
    vals = vals * np.repeat(np.exp2(scales.astype(np.float64) - 127.0), 8, axis=1)[..., None]
    return vals.transpose(0, 1, 3, 2).reshape(g * 512, n)


K, T, Z, J, R, C, O, N, E = 512, 1024, 1024, 256, 512, 512, 256, 256, 1024


def setup_inputs():
    n = np.random.standard_normal
    idx = np.random.permutation(T)[:J]
    idx2 = np.random.permutation(Z)[:J]
    idx3 = np.random.permutation(C)[:J]
    idx4 = np.random.permutation(C)[:J]
    idx5 = np.random.permutation(C)[:O]
    idx6 = np.random.permutation(C)[:O]
    idx7 = np.random.permutation(E)[:O]
    fk = mx_kscale(K)
    fr = mx_kscale(R)
    xtp = pack_weight(n((K, T)) / fk[:, None], "e5m2")
    xop = pack_weight(n((K, Z)) / fk[:, None], "e4m3")
    wp = pack_weight(n((K, R)) * 1 / np.sqrt(K) * fk[:, None] * fr, "e2m1")
    wbp = pack_weight(n((R, N)) * 1 / np.sqrt(R) / fr[:, None], "e2m1")
    return {
        "xt_words": xtp[0],
        "xt_scales": xtp[1],
        "xo_words": xop[0],
        "xo_scales": xop[1],
        "w_words": wp[0],
        "w_scales": wp[1],
        "wb_words": wbp[0],
        "wb_scales": wbp[1],
        "offs": striped(idx),
        "offs2": striped(idx2),
        "offs3": striped(idx3),
        "offs4": striped(idx4),
        "offs5": striped(idx5),
        "offs6": striped(idx6),
        "offs7": striped(idx7),
    }


def reference(xt_words, xt_scales, xo_words, xo_scales, w_words, w_scales, wb_words, wb_scales, offs, offs2, offs3, offs4, offs5, offs6, offs7):
    idx = unstriped(offs)
    idx2 = unstriped(offs2)
    idx3 = unstriped(offs3)
    idx4 = unstriped(offs4)
    idx5 = unstriped(offs5)
    idx6 = unstriped(offs6)
    idx7 = unstriped(offs7)
    xtu = unpack_weight(xt_words, xt_scales, "e5m2")
    xou = unpack_weight(xo_words, xo_scales, "e4m3")
    wu = unpack_weight(w_words, w_scales, "e2m1")
    wbu = unpack_weight(wb_words, wb_scales, "e2m1")
    xtidxg = xtu[:, idx]
    a = wu.T @ xtidxg
    xoidx2g = xou[:, idx2]
    b = wu.T @ xoidx2g
    pw = np.zeros((R, C))
    pw[:, idx3] = a
    pv = np.zeros((R, C))
    pv[:, idx4] = b
    hid = np.abs(pw[:, idx5] - pv[:, idx6])
    hidq = mxq(hid, 0, "e4m3")
    p = wbu.T @ hidq
    y = np.zeros((N, E))
    y[:, idx7] = p
    return y

@@ -1,0 +1,219 @@
+from contextlib import ExitStack
+
+import concourse.mybir as mybir
+
+K, T, J, R, C, O, N, E = 512, 1024, 256, 512, 512, 256, 256, 1024
+FLOPS = 2 * (2 * K * R * J) + 2 * R * N * O
+
+F32 = mybir.dt.float32
+BF16 = mybir.dt.bfloat16
+I32 = mybir.dt.int32
+U32 = mybir.dt.uint32
+U16 = mybir.dt.uint16
+U8 = mybir.dt.uint8
+E4M3 = mybir.dt.float8_e4m3fn_x4
+E5M2 = mybir.dt.float8_e5m2_x4
+E2M1 = mybir.dt.float4_e2m1fn_x4
+COPY = mybir.ActivationFunctionType.Copy
+ABS = mybir.ActivationFunctionType.Abs
+SUB = mybir.AluOpType.subtract
+
+P = 128
+PACK = 4
+HALVES = 2
+OH = O // HALVES
+LIST_COLS = J // 16
+
+
+def tile_list_oneforboth_twoboards_one_scattered_kernel(
+    tc, xt_words, xt_scales, xo_words, xo_scales, w_words, w_scales, wb_words, wb_scales,
+    offs, offs2, offs3, offs4, offs5, offs6, offs7, out,
+):
+    nc = tc.nc
+    with ExitStack() as ctx:
+        keep = ctx.enter_context(tc.tile_pool(name="keep", bufs=1))
+        psum = ctx.enter_context(tc.psum_pool(name="psum", bufs=1))
+
+        def load_list(name, src):
+            tile = keep.tile([P, LIST_COLS], U16, name=name)
+            nc.sync.dma_start(tile[:], src)
+            return tile
+
+        def load_words(name, src, dtype, cols):
+            tile = keep.tile([P, cols], dtype, name=name, align_bytes=64)
+            nc.sync.dma_start(tile[:].bitcast(I32), src.bitcast(I32))
+            return tile
+
+        def clear_plane(name, cols):
+            tile = keep.tile([P, cols], U8, name=name, align_bytes=64)
+            nc.vector.memset(tile[:].bitcast(I32), 0)
+            return tile
+
+        def load_plane(tile, src):
+            for q in range(4):
+                nc.sync.dma_start(tile[32 * q : 32 * q + 4, :].bitcast(I32), src[0, 4 * q : 4 * q + 4, :].bitcast(I32))
+
+        def load_plane_filled(name, src, cols):
+            tile = keep.tile([P, cols], U8, name=name, align_bytes=64)
+            for q in range(4):
+                rows = src[0, 4 * q : 4 * q + 4, :].bitcast(I32)
+                nc.sync.dma_start(tile[32 * q : 32 * q + 32, :].bitcast(I32), rows.partition_broadcast(8))
+            return tile
+
+        def scatter(on_vector, window, offsets, values):
+            if on_vector:
+                nc.vector.tensor_copy(window[:].indirect(offsets), values)
+            else:
+                nc.scalar.activation(window[:].indirect(offsets), values, COPY)
+
+        xo_plane = clear_plane("xo_plane", T)
+        wb_plane = clear_plane("wb_plane", N)
+
+        list_xt = load_list("list_xt", offs)
+        w_raw = load_words("w_raw", w_words[0], U8, 2 * R)
+        xt_table = load_words("xt_table", xt_words[0].rearrange("p n t -> p (n t)"), U32, T)
+        xt_plane = load_plane_filled("xt_plane", xt_scales, T)
+        w_plane = load_plane_filled("w_plane", w_scales, R)
+        list_put_a = load_list("list_put_a", offs3)
+        list_xo = load_list("list_xo", offs2)
+        xo_table = load_words("xo_table", xo_words[0].rearrange("p n t -> p (n t)"), U32, T)
+        load_plane(xo_plane, xo_scales)
+        list_get_pw = load_list("list_get_pw", offs5)
+        list_put_b = load_list("list_put_b", offs4)
+        list_get_pv = load_list("list_get_pv", offs6)
+        wb_codes = load_words("wb_codes", wb_words[0], U8, 2 * N)
+        load_plane(wb_plane, wb_scales)
+        list_put_p = load_list("list_put_p", offs7)
+
+        w_codes = keep.tile([P, 2 * R], U8, name="w_codes", align_bytes=64)
+        nc.vector.tensor_copy(
+            w_codes[:].bitcast(U16).rearrange("p (t m) -> p t m", t=PACK),
+            w_raw[:].bitcast(U16).rearrange("p (m t) -> p t m", t=PACK),
+        )
+
+        def pick(name, table, plane, offsets):
+            codes = keep.tile([P, J], U32, name=name + "_codes", align_bytes=64)
+            scales = keep.tile([P, J], U8, name=name + "_scales", align_bytes=64)
+            nc.vector.tensor_copy(codes[:], table[:].indirect(offsets[:]))
+            nc.vector.tensor_copy(scales[:], plane[:].indirect(offsets[:]))
+            return codes, scales
+
+        xt_codes, xt_sc = pick("xt", xt_table, xt_plane, list_xt)
+        w_sc = keep.tile([P, R], U8, name="w_sc", align_bytes=64)
+        nc.vector.tensor_copy(
+            w_sc[:].rearrange("p (t m) -> p t m", t=PACK),
+            w_plane[:].rearrange("p (m t) -> p t m", t=PACK),
+        )
+
+        def product(name, t, codes, scales, fmt, on_vector):
+            bank = psum.tile([P, 512], F32, name=name, tag=name)
+            nc.tensor.matmul_mx(
+                out=bank[:, 0:J],
+                lhsT=w_codes[:, 2 * P * t : 2 * P * (t + 1)].bitcast(E2M1),
+                lhsT_scale=w_sc[:, P * t : P * (t + 1)],
+                rhs=codes[:].bitcast(fmt),
+                rhs_scale=scales[:],
+                start=True,
+                stop=True,
+            )
+            values = keep.tile([P, J], F32, name=name + "_sb")
+            if on_vector:
+                nc.vector.tensor_copy(values[:], bank[:, 0:J])
+            else:
+                nc.scalar.copy(values[:], bank[:, 0:J])
+            return values
+
+        def board(name):
+            tile = keep.tile([P, C], F32, name=name)
+            nc.vector.memset(tile[:], 0.0)
+            return tile
+
+        pw = [board("pw%d" % t) for t in range(PACK)]
+        pv = [board("pv%d" % t) for t in range(PACK)]
+        a = [product("a%d" % t, t, xt_codes, xt_sc, E5M2, False) for t in range(PACK)]
+        xo_codes, xo_sc = pick("xo", xo_table, xo_plane, list_xo)
+        for t in range(PACK):
+            scatter(t % 2 == 1, pw[t], list_put_a[:], a[t][:])
+
+        pages = []
+        for name in ("xt_table", "xo_table"):
+            page = keep.tile([P, E], F32, name="page_" + name, tag=name, align_bytes=64)
+            nc.gpsimd.memset(page[:], 0.0)
+            pages.append(page)
+
+        diff = [keep.tile([P, PACK, OH], F32, name="diff%d" % h) for h in range(HALVES)]
+        picked_pw = [keep.tile([P, O], F32, name="picked_pw%d" % t) for t in range(PACK)]
+
+        def list_half(tile, h):
+            return tile[:, h * LIST_COLS // HALVES : (h + 1) * LIST_COLS // HALVES]
+
+        def fetch(t, h):
+            nc.scalar.activation(
+                picked_pw[t][:, h * OH : (h + 1) * OH], pw[t][:].indirect(list_half(list_get_pw, h)), COPY
+            )
+
+        def subtract(t, h):
+            nc.vector.tensor_tensor(
+                diff[h][:, t, :],
+                pv[t][:].indirect(list_half(list_get_pv, h)),
+                picked_pw[t][:, h * OH : (h + 1) * OH],
+                SUB,
+            )
+
+        def place_b(t):
+            values = product("b%d" % t, t, xo_codes, xo_sc, E4M3, t % 2 == 1)
+            scatter(t % 2 == 1, pv[t], list_put_b[:], values[:])
+
+        place_b(0)
+        place_b(1)
+        for t in range(PACK):
+            fetch(t, 0)
+        place_b(2)
+        place_b(3)
+        for t in (0, 1, 3, 2):
+            subtract(t, 0)
+
+        def head(h):
+            hid = keep.tile([P, OH, PACK], BF16, name="hid%d" % h, align_bytes=64)
+            nc.scalar.activation(
+                hid[:].rearrange("p (c i) t -> p c t i", i=4),
+                diff[h][:].rearrange("p t (c i) -> p c t i", i=4),
+                ABS,
+            )
+            codes = keep.tile([P, OH], U32, name="hid_codes%d" % h, align_bytes=64)
+            scales = keep.tile([P, OH], U8, name="hid_scales%d" % h, align_bytes=64)
+            nc.vector.quantize_mx(
+                out=codes[:].bitcast(E4M3), scales=scales[:], in_=hid[:].rearrange("p o t -> p (o t)")
+            )
+            return codes, scales
+
+        def tail(h, codes, scales):
+            cols = slice(h * LIST_COLS // HALVES, (h + 1) * LIST_COLS // HALVES)
+            for n in range(N // P):
+                tag = "a%d" % (2 * h + n)
+                bank = psum.tile([P, 512], F32, name="p%d%d" % (h, n), tag=tag)
+                nc.tensor.matmul_mx(
+                    out=bank[:, 0:OH],
+                    lhsT=wb_codes[:, 2 * P * n : 2 * P * (n + 1)].bitcast(E2M1),
+                    lhsT_scale=wb_plane[:, P * n : P * (n + 1)],
+                    rhs=codes[:].bitcast(E4M3),
+                    rhs_scale=scales[:],
+                    start=True,
+                    stop=True,
+                )
+                values = keep.tile([P, OH], F32, name="p_sb%d%d" % (h, n))
+                if n == 0:
+                    nc.vector.tensor_copy(values[:], bank[:, 0:OH])
+                else:
+                    nc.scalar.copy(values[:], bank[:, 0:OH])
+                scatter(n == 0, pages[n], list_put_p[:, cols], values[:])
+
+        first = head(0)
+        for t in range(PACK):
+            fetch(t, 1)
+            subtract(t, 1)
+        second = head(1)
+        tail(0, *first)
+        tail(1, *second)
+        nc.sync.dma_start(out[0:P, :], pages[0][:])
+        nc.scalar.dma_start(out[P : 2 * P, :], pages[1][:])

@@ -17,6 +17,8 @@ E2M1 = mybir.dt.float4_e2m1fn_x4
 COPY = mybir.ActivationFunctionType.Copy
 ABS = mybir.ActivationFunctionType.Abs
 SUB = mybir.AluOpType.subtract
+MULT = mybir.AluOpType.mult
+MAX = mybir.AluOpType.max
 
 P = 128
 PACK = 4
@@ -53,12 +55,9 @@ def tile_list_oneforboth_twoboards_one_scattered_kernel(
             for q in range(4):
                 nc.sync.dma_start(tile[32 * q : 32 * q + 4, :].bitcast(I32), src[0, 4 * q : 4 * q + 4, :].bitcast(I32))
 
-        def load_plane_filled(name, src, cols):
-            tile = keep.tile([P, cols], U8, name=name, align_bytes=64)
-            for q in range(4):
-                rows = src[0, 4 * q : 4 * q + 4, :].bitcast(I32)
-                nc.sync.dma_start(tile[32 * q : 32 * q + 32, :].bitcast(I32), rows.partition_broadcast(8))
-            return tile
+        def fill_quadrant(queue, tile, src, q):
+            rows = src[0, 4 * q : 4 * q + 4, :].bitcast(I32)
+            queue.dma_start(tile[32 * q : 32 * q + 32, :].bitcast(I32), rows.partition_broadcast(8))
 
         def scatter(on_vector, window, offsets, values):
             if on_vector:
@@ -69,20 +68,25 @@ def tile_list_oneforboth_twoboards_one_scattered_kernel(
         xo_plane = clear_plane("xo_plane", T)
         wb_plane = clear_plane("wb_plane", N)
 
+        xt_plane = keep.tile([P, T], U8, name="xt_plane", align_bytes=64)
+        w_plane = keep.tile([P, R], U8, name="w_plane", align_bytes=64)
         list_xt = load_list("list_xt", offs)
+        for q in range(4):
+            fill_quadrant(nc.scalar, xt_plane, xt_scales, q)
+        fill_quadrant(nc.sync, w_plane, w_scales, 0)
         w_raw = load_words("w_raw", w_words[0], U8, 2 * R)
         xt_table = load_words("xt_table", xt_words[0].rearrange("p n t -> p (n t)"), U32, T)
-        xt_plane = load_plane_filled("xt_plane", xt_scales, T)
-        w_plane = load_plane_filled("w_plane", w_scales, R)
-        list_put_a = load_list("list_put_a", offs3)
-        list_xo = load_list("list_xo", offs2)
+        for q in range(1, 4):
+            fill_quadrant(nc.sync, w_plane, w_scales, q)
         xo_table = load_words("xo_table", xo_words[0].rearrange("p n t -> p (n t)"), U32, T)
+        list_xo = load_list("list_xo", offs2)
         load_plane(xo_plane, xo_scales)
-        list_get_pw = load_list("list_get_pw", offs5)
-        list_put_b = load_list("list_put_b", offs4)
-        list_get_pv = load_list("list_get_pv", offs6)
+        list_put_a = load_list("list_put_a", offs3)
         wb_codes = load_words("wb_codes", wb_words[0], U8, 2 * N)
         load_plane(wb_plane, wb_scales)
+        list_put_b = load_list("list_put_b", offs4)
+        list_get_pw = load_list("list_get_pw", offs5)
+        list_get_pv = load_list("list_get_pv", offs6)
         list_put_p = load_list("list_put_p", offs7)
 
         w_codes = keep.tile([P, 2 * R], U8, name="w_codes", align_bytes=64)
@@ -94,18 +98,19 @@ def tile_list_oneforboth_twoboards_one_scattered_kernel(
         def pick(name, table, plane, offsets):
             codes = keep.tile([P, J], U32, name=name + "_codes", align_bytes=64)
             scales = keep.tile([P, J], U8, name=name + "_scales", align_bytes=64)
-            nc.vector.tensor_copy(codes[:], table[:].indirect(offsets[:]))
             nc.vector.tensor_copy(scales[:], plane[:].indirect(offsets[:]))
+            nc.vector.tensor_copy(codes[:], table[:].indirect(offsets[:]))
             return codes, scales
 
         xt_codes, xt_sc = pick("xt", xt_table, xt_plane, list_xt)
         w_sc = keep.tile([P, R], U8, name="w_sc", align_bytes=64)
-        nc.vector.tensor_copy(
-            w_sc[:].rearrange("p (t m) -> p t m", t=PACK),
-            w_plane[:].rearrange("p (m t) -> p t m", t=PACK),
-        )
+        for t in range(0, PACK, 2):
+            nc.vector.tensor_copy(
+                w_sc[:].rearrange("p (t m) -> p t m", t=PACK)[:, t : t + 2, :],
+                w_plane[:].rearrange("p (m t) -> p t m", t=PACK)[:, t : t + 2, :],
+            )
 
-        def product(name, t, codes, scales, fmt, on_vector):
+        def product(name, t, codes, scales, fmt, on_vector, tag):
             bank = psum.tile([P, 512], F32, name=name, tag=name)
             nc.tensor.matmul_mx(
                 out=bank[:, 0:J],
@@ -116,41 +121,43 @@ def tile_list_oneforboth_twoboards_one_scattered_kernel(
                 start=True,
                 stop=True,
             )
-            values = keep.tile([P, J], F32, name=name + "_sb")
+            values = keep.tile([P, J], F32, name=name + "_sb", tag=tag, align_bytes=64)
             if on_vector:
                 nc.vector.tensor_copy(values[:], bank[:, 0:J])
             else:
                 nc.scalar.copy(values[:], bank[:, 0:J])
             return values
 
-        def board(name):
-            tile = keep.tile([P, C], F32, name=name)
-            nc.vector.memset(tile[:], 0.0)
+        def cleared(engine, name, cols, tag):
+            tile = keep.tile([P, cols], F32, name=name, tag=tag, align_bytes=64)
+            engine.memset(tile[:], 0.0)
             return tile
 
-        pw = [board("pw%d" % t) for t in range(PACK)]
-        pv = [board("pv%d" % t) for t in range(PACK)]
-        a = [product("a%d" % t, t, xt_codes, xt_sc, E5M2, False) for t in range(PACK)]
+        pw = [cleared(nc.vector, "pw%d" % t, C, "pw%d" % t) for t in range(PACK)]
+        a = [product("a%d" % t, t, xt_codes, xt_sc, E5M2, False, "a%d_sb" % t) for t in range(PACK)]
         xo_codes, xo_sc = pick("xo", xo_table, xo_plane, list_xo)
         for t in range(PACK):
             scatter(t % 2 == 1, pw[t], list_put_a[:], a[t][:])
 
-        pages = []
-        for name in ("xt_table", "xo_table"):
-            page = keep.tile([P, E], F32, name="page_" + name, tag=name, align_bytes=64)
-            nc.gpsimd.memset(page[:], 0.0)
-            pages.append(page)
+        pv = [
+            cleared(nc.gpsimd, "pv%d" % t, C, tag)
+            for t, tag in enumerate(("w_plane", "xt_codes", "xt_scales", "xo_plane"))
+        ]
+        pages = [cleared(nc.gpsimd, "page%d" % n, E, tag) for n, tag in enumerate(("a1_sb", "xo_table"))]
 
-        diff = [keep.tile([P, PACK, OH], F32, name="diff%d" % h) for h in range(HALVES)]
+        diff = [keep.tile([P, PACK, OH], F32, name="diff%d" % h, align_bytes=64) for h in range(HALVES)]
         picked_pw = [keep.tile([P, O], F32, name="picked_pw%d" % t) for t in range(PACK)]
 
         def list_half(tile, h):
             return tile[:, h * LIST_COLS // HALVES : (h + 1) * LIST_COLS // HALVES]
 
         def fetch(t, h):
-            nc.scalar.activation(
-                picked_pw[t][:, h * OH : (h + 1) * OH], pw[t][:].indirect(list_half(list_get_pw, h)), COPY
-            )
+            picked = picked_pw[t][:, h * OH : (h + 1) * OH]
+            window = pw[t][:].indirect(list_half(list_get_pw, h))
+            if h == 0 and t % 2 == 1:
+                nc.vector.tensor_copy(picked, window)
+            else:
+                nc.scalar.activation(picked, window, COPY)
 
         def subtract(t, h):
             nc.vector.tensor_tensor(
@@ -160,26 +167,31 @@ def tile_list_oneforboth_twoboards_one_scattered_kernel(
                 SUB,
             )
 
-        def place_b(t):
-            values = product("b%d" % t, t, xo_codes, xo_sc, E4M3, t % 2 == 1)
-            scatter(t % 2 == 1, pv[t], list_put_b[:], values[:])
+        b = [product("b%d" % t, t, xo_codes, xo_sc, E4M3, t % 2 == 1, "b%d_sb" % t) for t in range(PACK)]
 
-        place_b(0)
-        place_b(1)
+        def place_b(t):
+            scatter(t % 2 == 1, pv[t], list_put_b[:], b[t][:])
+
         for t in range(PACK):
+            place_b(t)
+        for t in (1, 3, 0, 2):
             fetch(t, 0)
-        place_b(2)
-        place_b(3)
-        for t in (0, 1, 3, 2):
+        for t in (1, 3, 0, 2):
             subtract(t, 0)
 
-        def head(h):
+        def magnitude(h, split):
             hid = keep.tile([P, OH, PACK], BF16, name="hid%d" % h, align_bytes=64)
             nc.scalar.activation(
-                hid[:].rearrange("p (c i) t -> p c t i", i=4),
-                diff[h][:].rearrange("p t (c i) -> p c t i", i=4),
+                hid[:, 0:split, :].rearrange("p (c i) t -> p c t i", i=4),
+                diff[h][:, :, 0:split].rearrange("p t (c i) -> p c t i", i=4),
                 ABS,
             )
+            if split < OH:
+                rest = diff[h][:, :, split:OH].rearrange("p t o -> p o t")
+                nc.vector.scalar_tensor_tensor(hid[:, split:OH, :], rest, -1.0, rest, MULT, MAX)
+            return hid
+
+        def quantise(h, hid):
             codes = keep.tile([P, OH], U32, name="hid_codes%d" % h, align_bytes=64)
             scales = keep.tile([P, OH], U8, name="hid_scales%d" % h, align_bytes=64)
             nc.vector.quantize_mx(
@@ -187,33 +199,34 @@ def tile_list_oneforboth_twoboards_one_scattered_kernel(
             )
             return codes, scales
 
-        def tail(h, codes, scales):
-            cols = slice(h * LIST_COLS // HALVES, (h + 1) * LIST_COLS // HALVES)
-            for n in range(N // P):
-                tag = "a%d" % (2 * h + n)
-                bank = psum.tile([P, 512], F32, name="p%d%d" % (h, n), tag=tag)
-                nc.tensor.matmul_mx(
-                    out=bank[:, 0:OH],
-                    lhsT=wb_codes[:, 2 * P * n : 2 * P * (n + 1)].bitcast(E2M1),
-                    lhsT_scale=wb_plane[:, P * n : P * (n + 1)],
-                    rhs=codes[:].bitcast(E4M3),
-                    rhs_scale=scales[:],
-                    start=True,
-                    stop=True,
-                )
-                values = keep.tile([P, OH], F32, name="p_sb%d%d" % (h, n))
-                if n == 0:
-                    nc.vector.tensor_copy(values[:], bank[:, 0:OH])
-                else:
-                    nc.scalar.copy(values[:], bank[:, 0:OH])
-                scatter(n == 0, pages[n], list_put_p[:, cols], values[:])
+        def place_p(h, n, quantised, tag):
+            codes, scales = quantised
+            bank = psum.tile([P, 512], F32, name="p%d%d" % (h, n), tag="a%d" % (2 * h + n))
+            nc.tensor.matmul_mx(
+                out=bank[:, 0:OH],
+                lhsT=wb_codes[:, 2 * P * n : 2 * P * (n + 1)].bitcast(E2M1),
+                lhsT_scale=wb_plane[:, P * n : P * (n + 1)],
+                rhs=codes[:].bitcast(E4M3),
+                rhs_scale=scales[:],
+                start=True,
+                stop=True,
+            )
+            values = keep.tile([P, OH], F32, name="p_sb%d%d" % (h, n), tag=tag, align_bytes=64)
+            if n == 0:
+                nc.vector.tensor_copy(values[:], bank[:, 0:OH])
+            else:
+                nc.scalar.copy(values[:], bank[:, 0:OH])
+            scatter(n == 0, pages[n], list_half(list_put_p, h), values[:])
 
-        first = head(0)
-        for t in range(PACK):
+        first = quantise(0, magnitude(0, OH))
+        for t in (1, 3, 0, 2):
             fetch(t, 1)
             subtract(t, 1)
-        second = head(1)
-        tail(0, *first)
-        tail(1, *second)
+        hid_second = magnitude(1, 80)
+        place_p(0, 0, first, "p_sb00")
+        place_p(0, 1, first, "p_sb01")
+        second = quantise(1, hid_second)
+        place_p(1, 1, second, "p_sb11")
+        place_p(1, 0, second, "p_sb10")
         nc.sync.dma_start(out[0:P, :], pages[0][:])
         nc.scalar.dma_start(out[P : 2 * P, :], pages[1][:])

@@ -41,9 +41,9 @@ def tile_list_oneforboth_twoboards_one_scattered_kernel(
             nc.sync.dma_start(tile[:], src)
             return tile
 
-        def load_words(name, src, dtype, cols):
+        def load_words(queue, name, src, dtype, cols):
             tile = keep.tile([P, cols], dtype, name=name, align_bytes=64)
-            nc.sync.dma_start(tile[:].bitcast(I32), src.bitcast(I32))
+            queue.dma_start(tile[:].bitcast(I32), src.bitcast(I32))
             return tile
 
         def clear_plane(name, cols):
@@ -55,9 +55,9 @@ def tile_list_oneforboth_twoboards_one_scattered_kernel(
             for q in range(4):
                 nc.sync.dma_start(tile[32 * q : 32 * q + 4, :].bitcast(I32), src[0, 4 * q : 4 * q + 4, :].bitcast(I32))
 
-        def fill_quadrant(queue, tile, src, q):
+        def fill_quadrant(tile, src, q):
             rows = src[0, 4 * q : 4 * q + 4, :].bitcast(I32)
-            queue.dma_start(tile[32 * q : 32 * q + 32, :].bitcast(I32), rows.partition_broadcast(8))
+            nc.sync.dma_start(tile[32 * q : 32 * q + 32, :].bitcast(I32), rows.partition_broadcast(8))
 
         def scatter(on_vector, window, offsets, values):
             if on_vector:
@@ -71,18 +71,17 @@ def tile_list_oneforboth_twoboards_one_scattered_kernel(
         xt_plane = keep.tile([P, T], U8, name="xt_plane", align_bytes=64)
         w_plane = keep.tile([P, R], U8, name="w_plane", align_bytes=64)
         list_xt = load_list("list_xt", offs)
+        w_raw = load_words(nc.scalar, "w_raw", w_words[0], U8, 2 * R)
         for q in range(4):
-            fill_quadrant(nc.scalar, xt_plane, xt_scales, q)
-        fill_quadrant(nc.sync, w_plane, w_scales, 0)
-        w_raw = load_words("w_raw", w_words[0], U8, 2 * R)
-        xt_table = load_words("xt_table", xt_words[0].rearrange("p n t -> p (n t)"), U32, T)
-        for q in range(1, 4):
-            fill_quadrant(nc.sync, w_plane, w_scales, q)
-        xo_table = load_words("xo_table", xo_words[0].rearrange("p n t -> p (n t)"), U32, T)
+            fill_quadrant(xt_plane, xt_scales, q)
+        xt_table = load_words(nc.sync, "xt_table", xt_words[0].rearrange("p n t -> p (n t)"), U32, T)
+        for q in range(4):
+            fill_quadrant(w_plane, w_scales, q)
+        xo_table = load_words(nc.sync, "xo_table", xo_words[0].rearrange("p n t -> p (n t)"), U32, T)
         list_xo = load_list("list_xo", offs2)
         load_plane(xo_plane, xo_scales)
         list_put_a = load_list("list_put_a", offs3)
-        wb_codes = load_words("wb_codes", wb_words[0], U8, 2 * N)
+        wb_codes = load_words(nc.sync, "wb_codes", wb_words[0], U8, 2 * N)
         load_plane(wb_plane, wb_scales)
         list_put_b = load_list("list_put_b", offs4)
         list_get_pw = load_list("list_get_pw", offs5)
@@ -104,13 +103,13 @@ def tile_list_oneforboth_twoboards_one_scattered_kernel(
 
         xt_codes, xt_sc = pick("xt", xt_table, xt_plane, list_xt)
         w_sc = keep.tile([P, R], U8, name="w_sc", align_bytes=64)
-        for t in range(0, PACK, 2):
+        for t in (1, 0):
             nc.vector.tensor_copy(
-                w_sc[:].rearrange("p (t m) -> p t m", t=PACK)[:, t : t + 2, :],
-                w_plane[:].rearrange("p (m t) -> p t m", t=PACK)[:, t : t + 2, :],
+                w_sc[:].rearrange("p (t m) -> p t m", t=PACK)[:, t:PACK:2, :],
+                w_plane[:].rearrange("p (m t) -> p t m", t=PACK)[:, t:PACK:2, :],
             )
 
-        def product(name, t, codes, scales, fmt, on_vector, tag):
+        def product(name, t, codes, scales, fmt, on_vector, values):
             bank = psum.tile([P, 512], F32, name=name, tag=name)
             nc.tensor.matmul_mx(
                 out=bank[:, 0:J],
@@ -121,12 +120,10 @@ def tile_list_oneforboth_twoboards_one_scattered_kernel(
                 start=True,
                 stop=True,
             )
-            values = keep.tile([P, J], F32, name=name + "_sb", tag=tag, align_bytes=64)
             if on_vector:
-                nc.vector.tensor_copy(values[:], bank[:, 0:J])
+                nc.vector.tensor_copy(values, bank[:, 0:J])
             else:
-                nc.scalar.copy(values[:], bank[:, 0:J])
-            return values
+                nc.scalar.copy(values, bank[:, 0:J])
 
         def cleared(engine, name, cols, tag):
             tile = keep.tile([P, cols], F32, name=name, tag=tag, align_bytes=64)
@@ -134,16 +131,20 @@ def tile_list_oneforboth_twoboards_one_scattered_kernel(
             return tile
 
         pw = [cleared(nc.vector, "pw%d" % t, C, "pw%d" % t) for t in range(PACK)]
-        a = [product("a%d" % t, t, xt_codes, xt_sc, E5M2, False, "a%d_sb" % t) for t in range(PACK)]
         xo_codes, xo_sc = pick("xo", xo_table, xo_plane, list_xo)
+        a_even = keep.tile([P, 2, J], F32, name="a_even", align_bytes=64)
+        a_odd = keep.tile([P, 2, J], F32, name="a_odd", align_bytes=64)
+        a = [(a_even, a_odd)[t % 2][:, t // 2, :] for t in range(PACK)]
+        for t in (1, 3, 0, 2):
+            product("a%d" % t, t, xt_codes, xt_sc, E5M2, False, a[t])
         for t in range(PACK):
-            scatter(t % 2 == 1, pw[t], list_put_a[:], a[t][:])
+            scatter(t % 2 == 1, pw[t], list_put_a[:], a[t])
 
         pv = [
             cleared(nc.gpsimd, "pv%d" % t, C, tag)
             for t, tag in enumerate(("w_plane", "xt_codes", "xt_scales", "xo_plane"))
         ]
-        pages = [cleared(nc.gpsimd, "page%d" % n, E, tag) for n, tag in enumerate(("a1_sb", "xo_table"))]
+        pages = [cleared(nc.gpsimd, "page%d" % n, E, tag) for n, tag in enumerate(("a_even", "a_odd"))]
 
         diff = [keep.tile([P, PACK, OH], F32, name="diff%d" % h, align_bytes=64) for h in range(HALVES)]
         picked_pw = [keep.tile([P, O], F32, name="picked_pw%d" % t) for t in range(PACK)]
@@ -167,7 +168,9 @@ def tile_list_oneforboth_twoboards_one_scattered_kernel(
                 SUB,
             )
 
-        b = [product("b%d" % t, t, xo_codes, xo_sc, E4M3, t % 2 == 1, "b%d_sb" % t) for t in range(PACK)]
+        b = [keep.tile([P, J], F32, name="b%d_sb" % t, align_bytes=64) for t in range(PACK)]
+        for t in (1, 0, 3, 2):
+            product("b%d" % t, t, xo_codes, xo_sc, E4M3, t % 2 == 1, b[t][:])
 
         def place_b(t):
             scatter(t % 2 == 1, pv[t], list_put_b[:], b[t][:])

@@ -131,6 +131,7 @@ def tile_list_oneforboth_twoboards_one_scattered_kernel(
             return tile
 
         pw = [cleared(nc.vector, "pw%d" % t, C, "pw%d" % t) for t in range(PACK)]
+        pv = [cleared(nc.vector, "pv%d" % t, C, "pv%d" % t) for t in range(PACK)]
         xo_codes, xo_sc = pick("xo", xo_table, xo_plane, list_xo)
         a_even = keep.tile([P, 2, J], F32, name="a_even", align_bytes=64)
         a_odd = keep.tile([P, 2, J], F32, name="a_odd", align_bytes=64)
@@ -140,11 +141,6 @@ def tile_list_oneforboth_twoboards_one_scattered_kernel(
         for t in range(PACK):
             scatter(t % 2 == 1, pw[t], list_put_a[:], a[t])
 
-        pv = [
-            cleared(nc.gpsimd, "pv%d" % t, C, tag)
-            for t, tag in enumerate(("w_plane", "xt_codes", "xt_scales", "xo_plane"))
-        ]
-        pages = [cleared(nc.gpsimd, "page%d" % n, E, tag) for n, tag in enumerate(("a_even", "a_odd"))]
 
         diff = [keep.tile([P, PACK, OH], F32, name="diff%d" % h, align_bytes=64) for h in range(HALVES)]
         picked_pw = [keep.tile([P, O], F32, name="picked_pw%d" % t) for t in range(PACK)]
@@ -154,11 +150,7 @@ def tile_list_oneforboth_twoboards_one_scattered_kernel(
 
         def fetch(t, h):
             picked = picked_pw[t][:, h * OH : (h + 1) * OH]
-            window = pw[t][:].indirect(list_half(list_get_pw, h))
-            if h == 0 and t % 2 == 1:
-                nc.vector.tensor_copy(picked, window)
-            else:
-                nc.scalar.activation(picked, window, COPY)
+            nc.scalar.activation(picked, pw[t][:].indirect(list_half(list_get_pw, h)), COPY)
 
         def subtract(t, h):
             nc.vector.tensor_tensor(
@@ -177,6 +169,7 @@ def tile_list_oneforboth_twoboards_one_scattered_kernel(
 
         for t in range(PACK):
             place_b(t)
+        pages = [cleared(nc.gpsimd, "page%d" % n, E, "b%d_sb" % (PACK - 1 - n)) for n in range(N // P)]
         for t in (1, 3, 0, 2):
             fetch(t, 0)
         for t in (1, 3, 0, 2):

@@ -22,9 +22,16 @@ MAX = mybir.AluOpType.max
 
 P = 128
 PACK = 4
+QUADRANTS = 4
+QUAD = P // QUADRANTS
+SCALE_ROWS = 4
+BANK = 512
 HALVES = 2
 OH = O // HALVES
 LIST_COLS = J // 16
+LINE = 4
+ODD_FIRST = (1, 3, 0, 2)
+SCALAR_READS = 80
 
 
 def tile_list_oneforboth_twoboards_one_scattered_kernel(
@@ -51,13 +58,23 @@ def tile_list_oneforboth_twoboards_one_scattered_kernel(
             nc.vector.memset(tile[:].bitcast(I32), 0)
             return tile
 
-        def load_plane(tile, src):
-            for q in range(4):
-                nc.sync.dma_start(tile[32 * q : 32 * q + 4, :].bitcast(I32), src[0, 4 * q : 4 * q + 4, :].bitcast(I32))
+        def scale_rows(src, q):
+            return src[0, SCALE_ROWS * q : SCALE_ROWS * (q + 1), :].bitcast(I32)
 
-        def fill_quadrant(tile, src, q):
-            rows = src[0, 4 * q : 4 * q + 4, :].bitcast(I32)
-            nc.sync.dma_start(tile[32 * q : 32 * q + 32, :].bitcast(I32), rows.partition_broadcast(8))
+        def load_plane(tile, src):
+            for q in range(QUADRANTS):
+                nc.sync.dma_start(tile[QUAD * q : QUAD * q + SCALE_ROWS, :].bitcast(I32), scale_rows(src, q))
+
+        def load_plane_repeated(tile, src):
+            for q in range(QUADRANTS):
+                rows = scale_rows(src, q).partition_broadcast(QUAD // SCALE_ROWS)
+                nc.sync.dma_start(tile[QUAD * q : QUAD * (q + 1), :].bitcast(I32), rows)
+
+        def evacuate(on_vector, values, bank):
+            if on_vector:
+                nc.vector.tensor_copy(values, bank)
+            else:
+                nc.scalar.copy(values, bank)
 
         def scatter(on_vector, window, offsets, values):
             if on_vector:
@@ -65,26 +82,31 @@ def tile_list_oneforboth_twoboards_one_scattered_kernel(
             else:
                 nc.scalar.activation(window[:].indirect(offsets), values, COPY)
 
+        def cleared(engine, name, cols, tag):
+            tile = keep.tile([P, cols], F32, name=name, tag=tag, align_bytes=64)
+            engine.memset(tile[:], 0.0)
+            return tile
+
+        def list_half(tile, h):
+            return tile[:, h * LIST_COLS // HALVES : (h + 1) * LIST_COLS // HALVES]
+
         xo_plane = clear_plane("xo_plane", T)
         wb_plane = clear_plane("wb_plane", N)
-
         xt_plane = keep.tile([P, T], U8, name="xt_plane", align_bytes=64)
         w_plane = keep.tile([P, R], U8, name="w_plane", align_bytes=64)
         list_xt = load_list("list_xt", offs)
         w_raw = load_words(nc.scalar, "w_raw", w_words[0], U8, 2 * R)
-        for q in range(4):
-            fill_quadrant(xt_plane, xt_scales, q)
+        load_plane_repeated(xt_plane, xt_scales)
         xt_table = load_words(nc.sync, "xt_table", xt_words[0].rearrange("p n t -> p (n t)"), U32, T)
-        for q in range(4):
-            fill_quadrant(w_plane, w_scales, q)
+        load_plane_repeated(w_plane, w_scales)
         xo_table = load_words(nc.sync, "xo_table", xo_words[0].rearrange("p n t -> p (n t)"), U32, T)
         list_xo = load_list("list_xo", offs2)
         load_plane(xo_plane, xo_scales)
         list_put_a = load_list("list_put_a", offs3)
         wb_codes = load_words(nc.sync, "wb_codes", wb_words[0], U8, 2 * N)
         load_plane(wb_plane, wb_scales)
-        list_put_b = load_list("list_put_b", offs4)
         list_get_pw = load_list("list_get_pw", offs5)
+        list_put_b = load_list("list_put_b", offs4)
         list_get_pv = load_list("list_get_pv", offs6)
         list_put_p = load_list("list_put_p", offs7)
 
@@ -103,14 +125,14 @@ def tile_list_oneforboth_twoboards_one_scattered_kernel(
 
         xt_codes, xt_sc = pick("xt", xt_table, xt_plane, list_xt)
         w_sc = keep.tile([P, R], U8, name="w_sc", align_bytes=64)
-        for t in (1, 0):
+        for parity in (1, 0):
             nc.vector.tensor_copy(
-                w_sc[:].rearrange("p (t m) -> p t m", t=PACK)[:, t:PACK:2, :],
-                w_plane[:].rearrange("p (m t) -> p t m", t=PACK)[:, t:PACK:2, :],
+                w_sc[:].rearrange("p (t m) -> p t m", t=PACK)[:, parity:PACK:2, :],
+                w_plane[:].rearrange("p (m t) -> p t m", t=PACK)[:, parity:PACK:2, :],
             )
 
         def product(name, t, codes, scales, fmt, on_vector, values):
-            bank = psum.tile([P, 512], F32, name=name, tag=name)
+            bank = psum.tile([P, BANK], F32, name=name, tag=name)
             nc.tensor.matmul_mx(
                 out=bank[:, 0:J],
                 lhsT=w_codes[:, 2 * P * t : 2 * P * (t + 1)].bitcast(E2M1),
@@ -120,33 +142,22 @@ def tile_list_oneforboth_twoboards_one_scattered_kernel(
                 start=True,
                 stop=True,
             )
-            if on_vector:
-                nc.vector.tensor_copy(values, bank[:, 0:J])
-            else:
-                nc.scalar.copy(values, bank[:, 0:J])
-
-        def cleared(engine, name, cols, tag):
-            tile = keep.tile([P, cols], F32, name=name, tag=tag, align_bytes=64)
-            engine.memset(tile[:], 0.0)
-            return tile
+            evacuate(on_vector, values, bank[:, 0:J])
 
         pw = [cleared(nc.vector, "pw%d" % t, C, "pw%d" % t) for t in range(PACK)]
         pv = [cleared(nc.vector, "pv%d" % t, C, "pv%d" % t) for t in range(PACK)]
         xo_codes, xo_sc = pick("xo", xo_table, xo_plane, list_xo)
-        a_even = keep.tile([P, 2, J], F32, name="a_even", align_bytes=64)
-        a_odd = keep.tile([P, 2, J], F32, name="a_odd", align_bytes=64)
+
+        a_even = keep.tile([P, PACK // 2, J], F32, name="a_even", align_bytes=64)
+        a_odd = keep.tile([P, PACK // 2, J], F32, name="a_odd", align_bytes=64)
         a = [(a_even, a_odd)[t % 2][:, t // 2, :] for t in range(PACK)]
-        for t in (1, 3, 0, 2):
+        for t in ODD_FIRST:
             product("a%d" % t, t, xt_codes, xt_sc, E5M2, False, a[t])
         for t in range(PACK):
             scatter(t % 2 == 1, pw[t], list_put_a[:], a[t])
 
-
         diff = [keep.tile([P, PACK, OH], F32, name="diff%d" % h, align_bytes=64) for h in range(HALVES)]
         picked_pw = [keep.tile([P, O], F32, name="picked_pw%d" % t) for t in range(PACK)]
-
-        def list_half(tile, h):
-            return tile[:, h * LIST_COLS // HALVES : (h + 1) * LIST_COLS // HALVES]
 
         def fetch(t, h):
             picked = picked_pw[t][:, h * OH : (h + 1) * OH]
@@ -163,28 +174,25 @@ def tile_list_oneforboth_twoboards_one_scattered_kernel(
         b = [keep.tile([P, J], F32, name="b%d_sb" % t, align_bytes=64) for t in range(PACK)]
         for t in (1, 0, 3, 2):
             product("b%d" % t, t, xo_codes, xo_sc, E4M3, t % 2 == 1, b[t][:])
-
-        def place_b(t):
+        for t in range(PACK):
             scatter(t % 2 == 1, pv[t], list_put_b[:], b[t][:])
 
-        for t in range(PACK):
-            place_b(t)
-        pages = [cleared(nc.gpsimd, "page%d" % n, E, "b%d_sb" % (PACK - 1 - n)) for n in range(N // P)]
-        for t in (1, 3, 0, 2):
+        pages = [cleared(nc.vector, "page0", E, "w_plane"), cleared(nc.gpsimd, "page1", E, "b3_sb")]
+        for t in ODD_FIRST:
             fetch(t, 0)
-        for t in (1, 3, 0, 2):
+        for t in ODD_FIRST:
             subtract(t, 0)
 
-        def magnitude(h, split):
+        def magnitude(h, scalar_reads):
             hid = keep.tile([P, OH, PACK], BF16, name="hid%d" % h, align_bytes=64)
             nc.scalar.activation(
-                hid[:, 0:split, :].rearrange("p (c i) t -> p c t i", i=4),
-                diff[h][:, :, 0:split].rearrange("p t (c i) -> p c t i", i=4),
+                hid[:, 0:scalar_reads, :].rearrange("p (c i) t -> p c t i", i=LINE),
+                diff[h][:, :, 0:scalar_reads].rearrange("p t (c i) -> p c t i", i=LINE),
                 ABS,
             )
-            if split < OH:
-                rest = diff[h][:, :, split:OH].rearrange("p t o -> p o t")
-                nc.vector.scalar_tensor_tensor(hid[:, split:OH, :], rest, -1.0, rest, MULT, MAX)
+            if scalar_reads < OH:
+                rest = diff[h][:, :, scalar_reads:OH].rearrange("p t o -> p o t")
+                nc.vector.scalar_tensor_tensor(hid[:, scalar_reads:OH, :], rest, -1.0, rest, MULT, MAX)
             return hid
 
         def quantise(h, hid):
@@ -195,9 +203,9 @@ def tile_list_oneforboth_twoboards_one_scattered_kernel(
             )
             return codes, scales
 
-        def place_p(h, n, quantised, tag):
+        def place_p(h, n, quantised):
             codes, scales = quantised
-            bank = psum.tile([P, 512], F32, name="p%d%d" % (h, n), tag="a%d" % (2 * h + n))
+            bank = psum.tile([P, BANK], F32, name="p%d%d" % (h, n), tag="a%d" % (2 * h + n))
             nc.tensor.matmul_mx(
                 out=bank[:, 0:OH],
                 lhsT=wb_codes[:, 2 * P * n : 2 * P * (n + 1)].bitcast(E2M1),
@@ -207,22 +215,19 @@ def tile_list_oneforboth_twoboards_one_scattered_kernel(
                 start=True,
                 stop=True,
             )
-            values = keep.tile([P, OH], F32, name="p_sb%d%d" % (h, n), tag=tag, align_bytes=64)
-            if n == 0:
-                nc.vector.tensor_copy(values[:], bank[:, 0:OH])
-            else:
-                nc.scalar.copy(values[:], bank[:, 0:OH])
+            values = keep.tile([P, OH], F32, name="p_sb%d%d" % (h, n), align_bytes=64)
+            evacuate(n == 0, values[:], bank[:, 0:OH])
             scatter(n == 0, pages[n], list_half(list_put_p, h), values[:])
 
         first = quantise(0, magnitude(0, OH))
-        for t in (1, 3, 0, 2):
+        for t in ODD_FIRST:
             fetch(t, 1)
             subtract(t, 1)
-        hid_second = magnitude(1, 80)
-        place_p(0, 0, first, "p_sb00")
-        place_p(0, 1, first, "p_sb01")
+        hid_second = magnitude(1, SCALAR_READS)
+        place_p(0, 0, first)
+        place_p(0, 1, first)
         second = quantise(1, hid_second)
-        place_p(1, 1, second, "p_sb11")
-        place_p(1, 0, second, "p_sb10")
+        place_p(1, 1, second)
+        place_p(1, 0, second)
         nc.sync.dma_start(out[0:P, :], pages[0][:])
         nc.scalar.dma_start(out[P : 2 * P, :], pages[1][:])

from contextlib import ExitStack

import concourse.mybir as mybir

K, T, J, R, C, O, N, E = 512, 1024, 256, 512, 512, 256, 256, 1024
FLOPS = 2 * (2 * K * R * J) + 2 * R * N * O

F32 = mybir.dt.float32
BF16 = mybir.dt.bfloat16
I32 = mybir.dt.int32
U32 = mybir.dt.uint32
U16 = mybir.dt.uint16
U8 = mybir.dt.uint8
E4M3 = mybir.dt.float8_e4m3fn_x4
E5M2 = mybir.dt.float8_e5m2_x4
E2M1 = mybir.dt.float4_e2m1fn_x4
COPY = mybir.ActivationFunctionType.Copy
ABS = mybir.ActivationFunctionType.Abs
SUB = mybir.AluOpType.subtract
MULT = mybir.AluOpType.mult
MAX = mybir.AluOpType.max

P = 128
PACK = 4
QUADRANTS = 4
QUAD = P // QUADRANTS
SCALE_ROWS = 4
BANK = 512
HALVES = 2
OH = O // HALVES
LIST_COLS = J // 16
LINE = 4
ODD_FIRST = (1, 3, 0, 2)
SCALAR_READS = 80


def tile_list_oneforboth_twoboards_one_scattered_kernel(
    tc, xt_words, xt_scales, xo_words, xo_scales, w_words, w_scales, wb_words, wb_scales,
    offs, offs2, offs3, offs4, offs5, offs6, offs7, out,
):
    nc = tc.nc
    with ExitStack() as ctx:
        keep = ctx.enter_context(tc.tile_pool(name="keep", bufs=1))
        psum = ctx.enter_context(tc.psum_pool(name="psum", bufs=1))

        def load_list(name, src):
            tile = keep.tile([P, LIST_COLS], U16, name=name)
            nc.sync.dma_start(tile[:], src)
            return tile

        def load_words(queue, name, src, dtype, cols):
            tile = keep.tile([P, cols], dtype, name=name, align_bytes=64)
            queue.dma_start(tile[:].bitcast(I32), src.bitcast(I32))
            return tile

        def clear_plane(name, cols):
            tile = keep.tile([P, cols], U8, name=name, align_bytes=64)
            nc.vector.memset(tile[:].bitcast(I32), 0)
            return tile

        def scale_rows(src, q):
            return src[0, SCALE_ROWS * q : SCALE_ROWS * (q + 1), :].bitcast(I32)

        def load_plane(tile, src):
            for q in range(QUADRANTS):
                nc.sync.dma_start(tile[QUAD * q : QUAD * q + SCALE_ROWS, :].bitcast(I32), scale_rows(src, q))

        def load_plane_repeated(tile, src):
            for q in range(QUADRANTS):
                rows = scale_rows(src, q).partition_broadcast(QUAD // SCALE_ROWS)
                nc.sync.dma_start(tile[QUAD * q : QUAD * (q + 1), :].bitcast(I32), rows)

        def evacuate(on_vector, values, bank):
            if on_vector:
                nc.vector.tensor_copy(values, bank)
            else:
                nc.scalar.copy(values, bank)

        def scatter(on_vector, window, offsets, values):
            if on_vector:
                nc.vector.tensor_copy(window[:].indirect(offsets), values)
            else:
                nc.scalar.activation(window[:].indirect(offsets), values, COPY)

        def cleared(engine, name, cols, tag):
            tile = keep.tile([P, cols], F32, name=name, tag=tag, align_bytes=64)
            engine.memset(tile[:], 0.0)
            return tile

        def list_half(tile, h):
            return tile[:, h * LIST_COLS // HALVES : (h + 1) * LIST_COLS // HALVES]

        xo_plane = clear_plane("xo_plane", T)
        wb_plane = clear_plane("wb_plane", N)
        xt_plane = keep.tile([P, T], U8, name="xt_plane", align_bytes=64)
        w_plane = keep.tile([P, R], U8, name="w_plane", align_bytes=64)
        list_xt = load_list("list_xt", offs)
        w_raw = load_words(nc.scalar, "w_raw", w_words[0], U8, 2 * R)
        load_plane_repeated(xt_plane, xt_scales)
        xt_table = load_words(nc.sync, "xt_table", xt_words[0].rearrange("p n t -> p (n t)"), U32, T)
        load_plane_repeated(w_plane, w_scales)
        xo_table = load_words(nc.sync, "xo_table", xo_words[0].rearrange("p n t -> p (n t)"), U32, T)
        list_xo = load_list("list_xo", offs2)
        load_plane(xo_plane, xo_scales)
        list_put_a = load_list("list_put_a", offs3)
        wb_codes = load_words(nc.sync, "wb_codes", wb_words[0], U8, 2 * N)
        load_plane(wb_plane, wb_scales)
        list_get_pw = load_list("list_get_pw", offs5)
        list_put_b = load_list("list_put_b", offs4)
        list_get_pv = load_list("list_get_pv", offs6)
        list_put_p = load_list("list_put_p", offs7)

        w_codes = keep.tile([P, 2 * R], U8, name="w_codes", align_bytes=64)
        nc.vector.tensor_copy(
            w_codes[:].bitcast(U16).rearrange("p (t m) -> p t m", t=PACK),
            w_raw[:].bitcast(U16).rearrange("p (m t) -> p t m", t=PACK),
        )

        def pick(name, table, plane, offsets):
            codes = keep.tile([P, J], U32, name=name + "_codes", align_bytes=64)
            scales = keep.tile([P, J], U8, name=name + "_scales", align_bytes=64)
            nc.vector.tensor_copy(scales[:], plane[:].indirect(offsets[:]))
            nc.vector.tensor_copy(codes[:], table[:].indirect(offsets[:]))
            return codes, scales

        xt_codes, xt_sc = pick("xt", xt_table, xt_plane, list_xt)
        w_sc = keep.tile([P, R], U8, name="w_sc", align_bytes=64)
        for parity in (1, 0):
            nc.vector.tensor_copy(
                w_sc[:].rearrange("p (t m) -> p t m", t=PACK)[:, parity:PACK:2, :],
                w_plane[:].rearrange("p (m t) -> p t m", t=PACK)[:, parity:PACK:2, :],
            )

        def product(name, t, codes, scales, fmt, on_vector, values):
            bank = psum.tile([P, BANK], F32, name=name, tag=name)
            nc.tensor.matmul_mx(
                out=bank[:, 0:J],
                lhsT=w_codes[:, 2 * P * t : 2 * P * (t + 1)].bitcast(E2M1),
                lhsT_scale=w_sc[:, P * t : P * (t + 1)],
                rhs=codes[:].bitcast(fmt),
                rhs_scale=scales[:],
                start=True,
                stop=True,
            )
            evacuate(on_vector, values, bank[:, 0:J])

        pw = [cleared(nc.vector, "pw%d" % t, C, "pw%d" % t) for t in range(PACK)]
        pv = [cleared(nc.vector, "pv%d" % t, C, "pv%d" % t) for t in range(PACK)]
        xo_codes, xo_sc = pick("xo", xo_table, xo_plane, list_xo)

        a_even = keep.tile([P, PACK // 2, J], F32, name="a_even", align_bytes=64)
        a_odd = keep.tile([P, PACK // 2, J], F32, name="a_odd", align_bytes=64)
        a = [(a_even, a_odd)[t % 2][:, t // 2, :] for t in range(PACK)]
        for t in ODD_FIRST:
            product("a%d" % t, t, xt_codes, xt_sc, E5M2, False, a[t])
        for t in range(PACK):
            scatter(t % 2 == 1, pw[t], list_put_a[:], a[t])

        diff = [keep.tile([P, PACK, OH], F32, name="diff%d" % h, align_bytes=64) for h in range(HALVES)]
        picked_pw = [keep.tile([P, O], F32, name="picked_pw%d" % t) for t in range(PACK)]

        def fetch(t, h):
            picked = picked_pw[t][:, h * OH : (h + 1) * OH]
            nc.scalar.activation(picked, pw[t][:].indirect(list_half(list_get_pw, h)), COPY)

        def subtract(t, h):
            nc.vector.tensor_tensor(
                diff[h][:, t, :],
                pv[t][:].indirect(list_half(list_get_pv, h)),
                picked_pw[t][:, h * OH : (h + 1) * OH],
                SUB,
            )

        b = [keep.tile([P, J], F32, name="b%d_sb" % t, align_bytes=64) for t in range(PACK)]
        for t in (1, 0, 3, 2):
            product("b%d" % t, t, xo_codes, xo_sc, E4M3, t % 2 == 1, b[t][:])
        for t in range(PACK):
            scatter(t % 2 == 1, pv[t], list_put_b[:], b[t][:])

        pages = [cleared(nc.vector, "page0", E, "w_plane"), cleared(nc.gpsimd, "page1", E, "b3_sb")]
        for t in ODD_FIRST:
            fetch(t, 0)
        for t in ODD_FIRST:
            subtract(t, 0)

        def magnitude(h, scalar_reads):
            hid = keep.tile([P, OH, PACK], BF16, name="hid%d" % h, align_bytes=64)
            nc.scalar.activation(
                hid[:, 0:scalar_reads, :].rearrange("p (c i) t -> p c t i", i=LINE),
                diff[h][:, :, 0:scalar_reads].rearrange("p t (c i) -> p c t i", i=LINE),
                ABS,
            )
            if scalar_reads < OH:
                rest = diff[h][:, :, scalar_reads:OH].rearrange("p t o -> p o t")
                nc.vector.scalar_tensor_tensor(hid[:, scalar_reads:OH, :], rest, -1.0, rest, MULT, MAX)
            return hid

        def quantise(h, hid):
            codes = keep.tile([P, OH], U32, name="hid_codes%d" % h, align_bytes=64)
            scales = keep.tile([P, OH], U8, name="hid_scales%d" % h, align_bytes=64)
            nc.vector.quantize_mx(
                out=codes[:].bitcast(E4M3), scales=scales[:], in_=hid[:].rearrange("p o t -> p (o t)")
            )
            return codes, scales

        def place_p(h, n, quantised):
            codes, scales = quantised
            bank = psum.tile([P, BANK], F32, name="p%d%d" % (h, n), tag="a%d" % (2 * h + n))
            nc.tensor.matmul_mx(
                out=bank[:, 0:OH],
                lhsT=wb_codes[:, 2 * P * n : 2 * P * (n + 1)].bitcast(E2M1),
                lhsT_scale=wb_plane[:, P * n : P * (n + 1)],
                rhs=codes[:].bitcast(E4M3),
                rhs_scale=scales[:],
                start=True,
                stop=True,
            )
            values = keep.tile([P, OH], F32, name="p_sb%d%d" % (h, n), align_bytes=64)
            evacuate(n == 0, values[:], bank[:, 0:OH])
            scatter(n == 0, pages[n], list_half(list_put_p, h), values[:])

        first = quantise(0, magnitude(0, OH))
        for t in ODD_FIRST:
            fetch(t, 1)
            subtract(t, 1)
        hid_second = magnitude(1, SCALAR_READS)
        place_p(0, 0, first)
        place_p(0, 1, first)
        second = quantise(1, hid_second)
        place_p(1, 1, second)
        place_p(1, 0, second)
        nc.sync.dma_start(out[0:P, :], pages[0][:])
        nc.scalar.dma_start(out[P : 2 * P, :], pages[1][:])
